import numpy as np
import ml_dtypes


def mxq(x, axis, fmt="e4m3"):
    dtype, down = {"e4m3": (ml_dtypes.float8_e4m3fn, 7), "e5m2": (ml_dtypes.float8_e5m2, 14)}[fmt]
    v = np.moveaxis(np.asarray(x, np.float32).astype(ml_dtypes.bfloat16).astype(np.float64), axis, -1)
    blocks = v.reshape(v.shape[:-1] + (-1, 32))
    amax = np.abs(blocks).max(-1, keepdims=True)
    byte = np.maximum(np.where(amax > 0, np.frexp(amax)[1] - 1 + 127, 0) - down, 1)
    scale = np.exp2(byte - 127.0)
    codes = (blocks / scale).astype(np.float32).astype(dtype).astype(np.float64)
    return np.moveaxis((codes * scale).reshape(v.shape), -1, axis)


WIDE = False


def mx_kscale(k):
    if not WIDE:
        return np.ones(k)
    levels = np.array([10, -10, 5, -5, 0])
    if k % 512:
        return np.exp2(np.random.permutation(np.resize(levels, k // 32))).repeat(32)
    a = np.empty((k // 512, 16))
    for p in range(k // 512):
        a[p, :8] = np.random.permutation(np.resize(levels, 8))
        for g in range(8):
            far = levels[np.abs(levels - a[p, g]) >= 10]
            a[p, g + 8] = far[np.random.randint(len(far))]
    return np.exp2(a.ravel()).repeat(32)


def f64(x):
    return np.asarray(x).astype(np.float64)


def striped(idx):
    return np.tile(idx.reshape(-1, 16).T, (8, 1)).astype(np.uint16)


def unstriped(offs):
    return offs[:16].T.reshape(-1).astype(np.int64)


E2M1 = np.array([0.0, 0.5, 1.0, 1.5, 2.0, 3.0, 4.0, 6.0, -0.0, -0.5, -1.0, -1.5, -2.0, -3.0, -4.0, -6.0])


def pack_weight(w, fmt):
    k, n = w.shape
    w = f64(np.asarray(w, np.float32).astype(ml_dtypes.bfloat16)).reshape(k // 32, 32, n)
    amax = np.abs(w).max(1)
    if fmt == "e4m3":
        byte = np.frexp(amax)[1] - 1 + 127 - 7
    else:
        mant, ex = np.frexp(amax / 6.0)
        byte = np.where(mant > 0.5, ex, ex - 1) + 127
    byte = np.clip(np.where(amax > 0, byte, 1), 1, 254)
    scaled = (w * np.exp2(127.0 - byte)[:, None, :]).reshape(k, n).astype(np.float32)
    by_word = np.ascontiguousarray(scaled.reshape(k // 512, 128, 4, n).transpose(0, 1, 3, 2))
    if fmt == "e4m3":
        words = by_word.astype(ml_dtypes.float8_e4m3fn).view(np.uint8)
    else:
        c = by_word.astype(ml_dtypes.float4_e2m1fn).view(np.uint8) & 0xF
        words = (c[..., 0::2] | (c[..., 1::2] << 4)).reshape(k // 512, 128, 2 * n)
    return np.ascontiguousarray(words), np.ascontiguousarray(byte.astype(np.uint8).reshape(k // 512, 16, n))


def unpack_weight(words, scales, fmt):
    g, _, n = scales.shape
    words = np.ascontiguousarray(words).reshape(g, 128, n, -1)
    if fmt == "e4m3":
        vals = words.view(ml_dtypes.float8_e4m3fn).astype(np.float64)
    else:
        nib = np.empty((g, 128, n, 4), np.uint8)
        nib[..., 0::2] = words & 0xF
        nib[..., 1::2] = words >> 4
        vals = E2M1[nib]
    vals = vals * np.repeat(np.exp2(scales.astype(np.float64) - 127.0), 8, axis=1)[..., None]
    return vals.transpose(0, 1, 3, 2).reshape(g * 512, n)


def relu2(v):
    return np.maximum(v, 0.0) ** 2


K, T, E, C, N = 1024, 640, 4, 256, 512


def by_expert(wq, xq):
    return np.concatenate([wq[e].T @ xq[:, e * C:(e + 1) * C] for e in range(E)], axis=1)


def setup_inputs():
    n = np.random.standard_normal
    s = mx_kscale(K)[:, None]
    w = [pack_weight(m, "e2m1") for m in n((E, K, N)) / np.sqrt(K) / s[None]]
    idx = np.random.permutation(E * C)
    return {
        "xT": (n((K, T)) * s).astype(np.float32),
        "w_words": np.stack([m[0] for m in w]),
        "w_scales": np.stack([m[1] for m in w]),
        "b": (0.3 * n((N, E))).astype(np.float32),
        "gate": np.tile(np.where(idx < T, np.random.uniform(0.2, 1.0, E * C), 0.0), (N, 1)).astype(np.float32),
        "offs": striped(idx),
    }


def reference(xT, w_words, w_scales, b, gate, offs):
    idx = unstriped(offs)
    w = np.stack([unpack_weight(w_words[e], w_scales[e], "e2m1") for e in range(E)])
    xq = mxq(np.concatenate([f64(xT), np.zeros((K, E * C - T))], axis=1)[:, idx], 0, "e4m3")
    y = by_expert(w, xq)
    y = relu2(y + np.repeat(f64(b), C, axis=1))
    out = np.zeros((N, E * C))
    out[:, idx] = f64(gate) * y
    return out[:, :T]

@@ -1,0 +1,163 @@
+from contextlib import ExitStack
+
+import concourse.mybir as mybir
+
+K, T, E, C, N = 1024, 640, 4, 256, 512
+SLOTS = E * C
+FLOPS = 2 * K * N * SLOTS
+
+F32 = mybir.dt.float32
+BF16 = mybir.dt.bfloat16
+I32 = mybir.dt.int32
+U32 = mybir.dt.uint32
+U16 = mybir.dt.uint16
+U8 = mybir.dt.uint8
+FP8X4 = mybir.dt.float8_e4m3fn_x4
+FP4X4 = mybir.dt.float4_e2m1fn_x4
+ACT = mybir.ActivationFunctionType
+MULT = mybir.AluOpType.mult
+
+P = 128
+PACK = 4
+K_PASS = P * PACK
+PASSES = K // K_PASS
+BLOCKS = N // P
+PARTS = ((0, C), (C, SLOTS))
+GROUP = 128
+LIST_ROWS = 16
+SCALE_ROWS = 4
+CHUNKS = ((0, 384), (384, 640))
+QUANT = (((0, 256), (256, 384)), ((384, 640),))
+WIDE_WINDOW = 1536
+SHIFT_PARTS = 112
+
+
+def tile_moe_pad_lin_relu2_kernel(tc, xT, w_words, w_scales, b, gate, offs, out):
+    nc = tc.nc
+    with ExitStack() as ctx:
+        keep = ctx.enter_context(tc.tile_pool(name="keep", bufs=1))
+        psum = ctx.enter_context(tc.psum_pool(name="psum", bufs=2))
+
+        offsets = keep.tile([P, SLOTS // LIST_ROWS], U16, name="offsets")
+        nc.sync.dma_start(offsets[:], offs)
+
+        def listed(lo, hi):
+            return offsets[:, lo // LIST_ROWS : hi // LIST_ROWS]
+
+        w_scale = keep.tile([P, E * PASSES, N], U8, name="w_scale", align_bytes=64)
+        nc.vector.memset(w_scale[:].rearrange("p g n -> p (g n)").bitcast(I32), 0)
+        tok_scale = keep.tile([P, SLOTS], U8, name="tok_scale", align_bytes=64)
+        nc.vector.memset(tok_scale[:].bitcast(I32), 0)
+        tok_codes = [keep.tile([P, SLOTS], U32, name=f"tok_codes{a}", align_bytes=64) for a in range(PASSES)]
+        for a in range(PASSES):
+            nc.vector.memset(tok_codes[a][:, T:].bitcast(I32), 0)
+        moved_scale = [keep.tile([P, hi - lo], U8, name=f"moved_scale{h}", align_bytes=64) for h, (lo, hi) in enumerate(PARTS)]
+        for h in range(2):
+            nc.vector.memset(moved_scale[h][:].bitcast(I32), 0)
+        warm = keep.tile([P, 8], F32, name="warm")
+        nc.gpsimd.memset(warm[:], 0.0)
+        warm_out = keep.tile([P, 8], F32, name="warm_out")
+        nc.scalar.activation(warm_out[:], warm[:], ACT.Square)
+
+        raw = {}
+        for a in range(PASSES):
+            rows = xT[a * K_PASS : (a + 1) * K_PASS, :].rearrange("(p j) w -> p j w", j=PACK)
+            for i, (lo, hi) in enumerate(CHUNKS):
+                raw[a, i] = keep.tile([P, PACK, hi - lo], F32, name=f"raw{a}{i}")
+                nc.sync.dma_start(raw[a, i][:], rows[:, :, lo:hi])
+        for q in range(4):
+            nc.sync.dma_start(
+                w_scale[32 * q : 32 * q + SCALE_ROWS, :, :].bitcast(I32),
+                w_scales[:, :, SCALE_ROWS * q : SCALE_ROWS * (q + 1), :].rearrange("e a r n -> r (e a) n").bitcast(I32),
+            )
+        w_code = []
+        for h, (lo, hi) in enumerate(PARTS):
+            part = keep.tile([P, (hi - lo) // C * PASSES, 2 * N], U8, name=f"w_code{h}", align_bytes=64)
+            nc.sync.dma_start(
+                part[:].bitcast(I32),
+                w_words[lo // C : hi // C].rearrange("e a p n -> p (e a) n").bitcast(I32),
+            )
+            w_code.append(part)
+        bias = keep.tile([P, BLOCKS, 8], F32, name="bias")
+        nc.sync.dma_start(bias[:, :, 0:E], b.rearrange("(c p) e -> p c e", p=P))
+        gate_sb = keep.tile([P, SLOTS], F32, name="gate_sb")
+        nc.sync.dma_start(gate_sb[:], gate[0:P, :])
+
+        def weave(on_vector, dst, src):
+            dst_v = dst.rearrange("p (c i) t -> p c t i", i=4)
+            src_v = src.rearrange("p t (c i) -> p c t i", i=4)
+            if on_vector:
+                nc.vector.tensor_copy(dst_v, src_v)
+            else:
+                nc.scalar.activation(dst_v, src_v, ACT.Copy)
+
+        slot_codes = [[keep.tile([P, hi - lo], U32, name=f"slot_codes{a}{h}", align_bytes=64) for h, (lo, hi) in enumerate(PARTS)] for a in range(PASSES)]
+        slot_scale = [keep.tile([P, hi - lo], U8, name=f"slot_scale{h}", align_bytes=64) for h, (lo, hi) in enumerate(PARTS)]
+
+        def gather_codes(a, h):
+            nc.vector.tensor_copy(slot_codes[a][h][:], tok_codes[a][:].indirect(listed(*PARTS[h])))
+
+        for a in range(PASSES):
+            for i, (lo, hi) in enumerate(CHUNKS):
+                width = hi - lo
+                woven = keep.tile([P, width, PACK], BF16, name=f"woven{a}{i}", align_bytes=64)
+                if (a, i) == (0, 1):
+                    weave(True, woven[:, 0:160, :], raw[a, i][:, :, 0:160])
+                    weave(False, woven[:, 160:width, :], raw[a, i][:, :, 160:width])
+                else:
+                    weave((a, i) != (1, 0), woven[:], raw[a, i][:])
+                for q_lo, q_hi in QUANT[i]:
+                    nc.vector.quantize_mx(
+                        out=tok_codes[a][:, q_lo:q_hi].bitcast(FP8X4),
+                        scales=tok_scale[SCALE_ROWS * a : P, q_lo:q_hi],
+                        in_=woven[:, q_lo - lo : q_hi - lo, :].rearrange("p w t -> p (w t)"),
+                    )
+            if a == 0:
+                gather_codes(0, 0)
+                gather_codes(0, 1)
+
+        for h in range(2):
+            nc.vector.tensor_copy(slot_scale[h][:], tok_scale[:].indirect(listed(*PARTS[h])))
+            nc.scalar.dma_start(
+                moved_scale[h][0:SHIFT_PARTS, :].bitcast(I32),
+                slot_scale[h][SCALE_ROWS : SCALE_ROWS + SHIFT_PARTS, :].bitcast(I32),
+            )
+        for h in range(2):
+            gather_codes(1, h)
+
+        squared = [[keep.tile([P, hi - lo], F32, name=f"squared{c}{h}") for h, (lo, hi) in enumerate(PARTS)] for c in range(BLOCKS)]
+        windows = [keep.tile([P, WIDE_WINDOW], F32, name=f"window{c}") for c in range(BLOCKS)]
+
+        def expert(e, c):
+            h = min(e, 1)
+            first = e * C - PARTS[h][0]
+            bank = psum.tile([P, C], F32, name="bank")
+            relu = keep.tile([P, C], F32, name=f"relu{e}{c}")
+            for s in range(0, C, GROUP):
+                cols = slice(first + s, first + s + GROUP)
+                for a in range(PASSES):
+                    scales = slot_scale[h] if a == 0 else moved_scale[h]
+                    nc.tensor.matmul_mx(
+                        out=bank[:, s : s + GROUP],
+                        lhsT=w_code[h][:, first // C * PASSES + a, 2 * P * c : 2 * P * (c + 1)].bitcast(FP4X4),
+                        lhsT_scale=w_scale[:, e * PASSES + a, P * c : P * (c + 1)],
+                        rhs=slot_codes[a][h][:, cols].bitcast(FP8X4),
+                        rhs_scale=scales[:, cols],
+                        start=(a == 0),
+                        stop=(a == PASSES - 1),
+                    )
+            nc.scalar.activation(relu[:], bank[:], ACT.Relu, bias=bias[:, c, e : e + 1])
+            nc.scalar.activation(squared[c][h][:, first : first + C], relu[:], ACT.Square)
+
+        def scatter(c, h):
+            lo, hi = PARTS[h]
+            nc.vector.tensor_tensor(windows[c][:].indirect(listed(lo, hi)), squared[c][h][:], gate_sb[:, lo:hi], MULT)
+
+        for c in range(BLOCKS):
+            expert(0, c)
+            scatter(c, 0)
+        for c in range(BLOCKS):
+            for e in range(1, E):
+                expert(e, c)
+            scatter(c, 1)
+            nc.sync.dma_start(out[c * P : (c + 1) * P, :], windows[c][:, 0:T])

@@ -26,8 +26,8 @@ PARTS = ((0, C), (C, SLOTS))
 GROUP = 128
 LIST_ROWS = 16
 SCALE_ROWS = 4
-CHUNKS = ((0, 384), (384, 640))
-QUANT = (((0, 256), (256, 384)), ((384, 640),))
+CHUNKS = ((0, 256), (256, 512), (512, 640))
+ON_VECTOR = ((True, True, False), (False, False, True))
 WIDE_WINDOW = 1536
 SHIFT_PARTS = 112
 
@@ -36,19 +36,18 @@ def tile_moe_pad_lin_relu2_kernel(tc, xT, w_words, w_scales, b, gate, offs, out)
     nc = tc.nc
     with ExitStack() as ctx:
         keep = ctx.enter_context(tc.tile_pool(name="keep", bufs=1))
-        psum = ctx.enter_context(tc.psum_pool(name="psum", bufs=2))
+        psum = ctx.enter_context(tc.psum_pool(name="psum", bufs=3))
 
         offsets = keep.tile([P, SLOTS // LIST_ROWS], U16, name="offsets")
-        nc.sync.dma_start(offsets[:], offs)
 
         def listed(lo, hi):
             return offsets[:, lo // LIST_ROWS : hi // LIST_ROWS]
 
         w_scale = keep.tile([P, E * PASSES, N], U8, name="w_scale", align_bytes=64)
         nc.vector.memset(w_scale[:].rearrange("p g n -> p (g n)").bitcast(I32), 0)
-        tok_scale = keep.tile([P, SLOTS], U8, name="tok_scale", align_bytes=64)
+        tok_scale = keep.tile([P, SLOTS], U8, name="tok_scale", tag="then_weights", align_bytes=64)
         nc.vector.memset(tok_scale[:].bitcast(I32), 0)
-        tok_codes = [keep.tile([P, SLOTS], U32, name=f"tok_codes{a}", align_bytes=64) for a in range(PASSES)]
+        tok_codes = [keep.tile([P, SLOTS], U32, name=f"tok_codes{a}", tag=f"then_gate{a}", align_bytes=64) for a in range(PASSES)]
         for a in range(PASSES):
             nc.vector.memset(tok_codes[a][:, T:].bitcast(I32), 0)
         moved_scale = [keep.tile([P, hi - lo], U8, name=f"moved_scale{h}", align_bytes=64) for h, (lo, hi) in enumerate(PARTS)]
@@ -65,23 +64,32 @@ def tile_moe_pad_lin_relu2_kernel(tc, xT, w_words, w_scales, b, gate, offs, out)
             for i, (lo, hi) in enumerate(CHUNKS):
                 raw[a, i] = keep.tile([P, PACK, hi - lo], F32, name=f"raw{a}{i}")
                 nc.sync.dma_start(raw[a, i][:], rows[:, :, lo:hi])
+            if a == 0:
+                nc.sync.dma_start(offsets[:], offs)
         for q in range(4):
             nc.sync.dma_start(
                 w_scale[32 * q : 32 * q + SCALE_ROWS, :, :].bitcast(I32),
                 w_scales[:, :, SCALE_ROWS * q : SCALE_ROWS * (q + 1), :].rearrange("e a r n -> r (e a) n").bitcast(I32),
             )
-        w_code = []
-        for h, (lo, hi) in enumerate(PARTS):
-            part = keep.tile([P, (hi - lo) // C * PASSES, 2 * N], U8, name=f"w_code{h}", align_bytes=64)
+        w_code, gate_sb = {}, {}
+
+        def load_weights(h, tag):
+            lo, hi = PARTS[h]
+            w_code[h] = keep.tile([P, (hi - lo) // C * PASSES, 2 * N], U8, name=f"w_code{h}", tag=tag, align_bytes=64)
             nc.sync.dma_start(
-                part[:].bitcast(I32),
+                w_code[h][:].bitcast(I32),
                 w_words[lo // C : hi // C].rearrange("e a p n -> p (e a) n").bitcast(I32),
             )
-            w_code.append(part)
+
+        def load_gate(h, tag):
+            lo, hi = PARTS[h]
+            gate_sb[h] = keep.tile([P, hi - lo], F32, name=f"gate{h}", tag=tag, align_bytes=64)
+            nc.sync.dma_start(gate_sb[h][:], gate[0:P, lo:hi])
+
+        load_weights(0, "w_first")
         bias = keep.tile([P, BLOCKS, 8], F32, name="bias")
         nc.sync.dma_start(bias[:, :, 0:E], b.rearrange("(c p) e -> p c e", p=P))
-        gate_sb = keep.tile([P, SLOTS], F32, name="gate_sb")
-        nc.sync.dma_start(gate_sb[:], gate[0:P, :])
+        load_gate(0, "gate_first")
 
         def weave(on_vector, dst, src):
             dst_v = dst.rearrange("p (c i) t -> p c t i", i=4)
@@ -101,29 +109,33 @@ def tile_moe_pad_lin_relu2_kernel(tc, xT, w_words, w_scales, b, gate, offs, out)
             for i, (lo, hi) in enumerate(CHUNKS):
                 width = hi - lo
                 woven = keep.tile([P, width, PACK], BF16, name=f"woven{a}{i}", align_bytes=64)
-                if (a, i) == (0, 1):
-                    weave(True, woven[:, 0:160, :], raw[a, i][:, :, 0:160])
-                    weave(False, woven[:, 160:width, :], raw[a, i][:, :, 160:width])
-                else:
-                    weave((a, i) != (1, 0), woven[:], raw[a, i][:])
-                for q_lo, q_hi in QUANT[i]:
-                    nc.vector.quantize_mx(
-                        out=tok_codes[a][:, q_lo:q_hi].bitcast(FP8X4),
-                        scales=tok_scale[SCALE_ROWS * a : P, q_lo:q_hi],
-                        in_=woven[:, q_lo - lo : q_hi - lo, :].rearrange("p w t -> p (w t)"),
-                    )
+                weave(ON_VECTOR[a][i], woven[:], raw[a, i][:])
+                nc.vector.quantize_mx(
+                    out=tok_codes[a][:, lo:hi].bitcast(FP8X4),
+                    scales=tok_scale[SCALE_ROWS * a : P, lo:hi],
+                    in_=woven[:].rearrange("p w t -> p (w t)"),
+                )
             if a == 0:
                 gather_codes(0, 0)
                 gather_codes(0, 1)
 
         for h in range(2):
             nc.vector.tensor_copy(slot_scale[h][:], tok_scale[:].indirect(listed(*PARTS[h])))
-            nc.scalar.dma_start(
-                moved_scale[h][0:SHIFT_PARTS, :].bitcast(I32),
-                slot_scale[h][SCALE_ROWS : SCALE_ROWS + SHIFT_PARTS, :].bitcast(I32),
-            )
+            if h == 0:
+                for q in range(4):
+                    nc.scalar.dma_start(
+                        moved_scale[h][32 * q : 32 * q + SCALE_ROWS, :].bitcast(I32),
+                        slot_scale[h][32 * q + SCALE_ROWS : 32 * q + 2 * SCALE_ROWS, :].bitcast(I32),
+                    )
+            else:
+                nc.sync.dma_start(
+                    moved_scale[h][0:SHIFT_PARTS, :].bitcast(I32),
+                    slot_scale[h][SCALE_ROWS : SCALE_ROWS + SHIFT_PARTS, :].bitcast(I32),
+                )
+        load_weights(1, "then_weights")
         for h in range(2):
             gather_codes(1, h)
+        load_gate(1, "then_gate1")
 
         squared = [[keep.tile([P, hi - lo], F32, name=f"squared{c}{h}") for h, (lo, hi) in enumerate(PARTS)] for c in range(BLOCKS)]
         windows = [keep.tile([P, WIDE_WINDOW], F32, name=f"window{c}") for c in range(BLOCKS)]
@@ -131,14 +143,16 @@ def tile_moe_pad_lin_relu2_kernel(tc, xT, w_words, w_scales, b, gate, offs, out)
         def expert(e, c):
             h = min(e, 1)
             first = e * C - PARTS[h][0]
-            bank = psum.tile([P, C], F32, name="bank")
+            width = GROUP if (e, c) == (0, 0) else C
             relu = keep.tile([P, C], F32, name=f"relu{e}{c}")
             for s in range(0, C, GROUP):
+                if s % width == 0:
+                    bank = psum.tile([P, width], F32, name=f"bank{width}")
                 cols = slice(first + s, first + s + GROUP)
                 for a in range(PASSES):
                     scales = slot_scale[h] if a == 0 else moved_scale[h]
                     nc.tensor.matmul_mx(
-                        out=bank[:, s : s + GROUP],
+                        out=bank[:, s % width : s % width + GROUP],
                         lhsT=w_code[h][:, first // C * PASSES + a, 2 * P * c : 2 * P * (c + 1)].bitcast(FP4X4),
                         lhsT_scale=w_scale[:, e * PASSES + a, P * c : P * (c + 1)],
                         rhs=slot_codes[a][h][:, cols].bitcast(FP8X4),
@@ -146,12 +160,15 @@ def tile_moe_pad_lin_relu2_kernel(tc, xT, w_words, w_scales, b, gate, offs, out)
                         start=(a == 0),
                         stop=(a == PASSES - 1),
                     )
-            nc.scalar.activation(relu[:], bank[:], ACT.Relu, bias=bias[:, c, e : e + 1])
+                if (s + GROUP) % width == 0:
+                    nc.scalar.activation(
+                        relu[:, s + GROUP - width : s + GROUP], bank[:], ACT.Relu, bias=bias[:, c, e : e + 1]
+                    )
             nc.scalar.activation(squared[c][h][:, first : first + C], relu[:], ACT.Square)
 
         def scatter(c, h):
             lo, hi = PARTS[h]
-            nc.vector.tensor_tensor(windows[c][:].indirect(listed(lo, hi)), squared[c][h][:], gate_sb[:, lo:hi], MULT)
+            nc.vector.tensor_tensor(windows[c][:].indirect(listed(lo, hi)), squared[c][h][:], gate_sb[h][:], MULT)
 
         for c in range(BLOCKS):
             expert(0, c)

@@ -18,25 +18,31 @@ ACT = mybir.ActivationFunctionType
 MULT = mybir.AluOpType.mult
 
 P = 128
+QUADRANT = 32
+SCALE_ROWS = 4
 PACK = 4
 K_PASS = P * PACK
 PASSES = K // K_PASS
 BLOCKS = N // P
-PARTS = ((0, C), (C, SLOTS))
 GROUP = 128
 LIST_ROWS = 16
-SCALE_ROWS = 4
+LINE = 4
+BIAS_PITCH = 8
+
 CHUNKS = ((0, 256), (256, 512), (512, 640))
-ON_VECTOR = ((True, True, False), (False, False, True))
-WIDE_WINDOW = 1536
-SHIFT_PARTS = 112
+VECTOR_TOKENS = ((256, 128, 64), (0, 64, 128))
+PARTS = ((0, C), (C, SLOTS))
+CODE_PARTS = (((0, 3 * C), (3 * C, SLOTS)), PARTS)
+WINDOW = 2 * (SLOTS - C)
+MOVE_PARTITIONS = 112
+PSUM_BUFS = 3
 
 
 def tile_moe_pad_lin_relu2_kernel(tc, xT, w_words, w_scales, b, gate, offs, out):
     nc = tc.nc
     with ExitStack() as ctx:
         keep = ctx.enter_context(tc.tile_pool(name="keep", bufs=1))
-        psum = ctx.enter_context(tc.psum_pool(name="psum", bufs=3))
+        psum = ctx.enter_context(tc.psum_pool(name="psum", bufs=PSUM_BUFS))
 
         offsets = keep.tile([P, SLOTS // LIST_ROWS], U16, name="offsets")
 
@@ -45,14 +51,19 @@ def tile_moe_pad_lin_relu2_kernel(tc, xT, w_words, w_scales, b, gate, offs, out)
 
         w_scale = keep.tile([P, E * PASSES, N], U8, name="w_scale", align_bytes=64)
         nc.vector.memset(w_scale[:].rearrange("p g n -> p (g n)").bitcast(I32), 0)
-        tok_scale = keep.tile([P, SLOTS], U8, name="tok_scale", tag="then_weights", align_bytes=64)
+        tok_scale = keep.tile([P, SLOTS], U8, name="tok_scale", tag="tok_scale", align_bytes=64)
         nc.vector.memset(tok_scale[:].bitcast(I32), 0)
-        tok_codes = [keep.tile([P, SLOTS], U32, name=f"tok_codes{a}", tag=f"then_gate{a}", align_bytes=64) for a in range(PASSES)]
+        tok_codes = [
+            keep.tile([P, SLOTS], U32, name=f"tok_codes{a}", tag=f"tok_codes{a}", align_bytes=64) for a in range(PASSES)
+        ]
         for a in range(PASSES):
             nc.vector.memset(tok_codes[a][:, T:].bitcast(I32), 0)
-        moved_scale = [keep.tile([P, hi - lo], U8, name=f"moved_scale{h}", align_bytes=64) for h, (lo, hi) in enumerate(PARTS)]
-        for h in range(2):
+        moved_scale = [
+            keep.tile([P, hi - lo], U8, name=f"moved_scale{h}", align_bytes=64) for h, (lo, hi) in enumerate(PARTS)
+        ]
+        for h in range(len(PARTS)):
             nc.vector.memset(moved_scale[h][:].bitcast(I32), 0)
+
         warm = keep.tile([P, 8], F32, name="warm")
         nc.gpsimd.memset(warm[:], 0.0)
         warm_out = keep.tile([P, 8], F32, name="warm_out")
@@ -60,17 +71,18 @@ def tile_moe_pad_lin_relu2_kernel(tc, xT, w_words, w_scales, b, gate, offs, out)
 
         raw = {}
         for a in range(PASSES):
-            rows = xT[a * K_PASS : (a + 1) * K_PASS, :].rearrange("(p j) w -> p j w", j=PACK)
+            rows = xT[a * K_PASS : (a + 1) * K_PASS, :].rearrange("(p d) t -> p d t", d=PACK)
             for i, (lo, hi) in enumerate(CHUNKS):
                 raw[a, i] = keep.tile([P, PACK, hi - lo], F32, name=f"raw{a}{i}")
                 nc.sync.dma_start(raw[a, i][:], rows[:, :, lo:hi])
             if a == 0:
                 nc.sync.dma_start(offsets[:], offs)
-        for q in range(4):
+        for r in range(SCALE_ROWS):
             nc.sync.dma_start(
-                w_scale[32 * q : 32 * q + SCALE_ROWS, :, :].bitcast(I32),
-                w_scales[:, :, SCALE_ROWS * q : SCALE_ROWS * (q + 1), :].rearrange("e a r n -> r (e a) n").bitcast(I32),
+                w_scale[r:P:QUADRANT, :, :].bitcast(I32),
+                w_scales.rearrange("e a (q r) n -> r q (e a) n", r=SCALE_ROWS)[r].bitcast(I32),
             )
+
         w_code, gate_sb = {}, {}
 
         def load_weights(h, tag):
@@ -86,95 +98,107 @@ def tile_moe_pad_lin_relu2_kernel(tc, xT, w_words, w_scales, b, gate, offs, out)
             gate_sb[h] = keep.tile([P, hi - lo], F32, name=f"gate{h}", tag=tag, align_bytes=64)
             nc.sync.dma_start(gate_sb[h][:], gate[0:P, lo:hi])
 
-        load_weights(0, "w_first")
-        bias = keep.tile([P, BLOCKS, 8], F32, name="bias")
+        load_weights(0, "w_code0")
+        bias = keep.tile([P, BLOCKS, BIAS_PITCH], F32, name="bias")
         nc.sync.dma_start(bias[:, :, 0:E], b.rearrange("(c p) e -> p c e", p=P))
-        load_gate(0, "gate_first")
+        load_gate(0, "gate0")
 
         def weave(on_vector, dst, src):
-            dst_v = dst.rearrange("p (c i) t -> p c t i", i=4)
-            src_v = src.rearrange("p t (c i) -> p c t i", i=4)
+            dst_view = dst.rearrange("p (g i) d -> p g d i", i=LINE)
+            src_view = src.rearrange("p d (g i) -> p g d i", i=LINE)
             if on_vector:
-                nc.vector.tensor_copy(dst_v, src_v)
+                nc.vector.tensor_copy(dst_view, src_view)
             else:
-                nc.scalar.activation(dst_v, src_v, ACT.Copy)
+                nc.scalar.activation(dst_view, src_view, ACT.Copy)
 
-        slot_codes = [[keep.tile([P, hi - lo], U32, name=f"slot_codes{a}{h}", align_bytes=64) for h, (lo, hi) in enumerate(PARTS)] for a in range(PASSES)]
-        slot_scale = [keep.tile([P, hi - lo], U8, name=f"slot_scale{h}", align_bytes=64) for h, (lo, hi) in enumerate(PARTS)]
+        slot_codes = {}
+        slot_scale = [
+            keep.tile([P, hi - lo], U8, name=f"slot_scale{h}", align_bytes=64) for h, (lo, hi) in enumerate(PARTS)
+        ]
 
-        def gather_codes(a, h):
-            nc.vector.tensor_copy(slot_codes[a][h][:], tok_codes[a][:].indirect(listed(*PARTS[h])))
+        def gather_codes(a, h, tag):
+            lo, hi = CODE_PARTS[a][h]
+            slot_codes[a, h] = keep.tile([P, hi - lo], U32, name=f"slot_codes{a}{h}", tag=tag, align_bytes=64)
+            nc.vector.tensor_copy(slot_codes[a, h][:], tok_codes[a][:].indirect(listed(lo, hi)))
+
+        def gather_scales(h):
+            nc.vector.tensor_copy(slot_scale[h][:], tok_scale[:].indirect(listed(*PARTS[h])))
+
+        def codes_of(a, slot):
+            h = 0 if slot < CODE_PARTS[a][0][1] else 1
+            first = slot - CODE_PARTS[a][h][0]
+            return slot_codes[a, h][:, first : first + GROUP]
 
         for a in range(PASSES):
             for i, (lo, hi) in enumerate(CHUNKS):
-                width = hi - lo
-                woven = keep.tile([P, width, PACK], BF16, name=f"woven{a}{i}", align_bytes=64)
-                weave(ON_VECTOR[a][i], woven[:], raw[a, i][:])
+                width, cut = hi - lo, VECTOR_TOKENS[a][i]
+                woven = keep.tile([P, width, PACK], BF16, name=f"woven{a}{i}", tag=f"woven{a}{i}", align_bytes=64)
+                if cut > 0:
+                    weave(True, woven[:, 0:cut, :], raw[a, i][:, :, 0:cut])
+                if cut < width:
+                    weave(False, woven[:, cut:width, :], raw[a, i][:, :, cut:width])
                 nc.vector.quantize_mx(
                     out=tok_codes[a][:, lo:hi].bitcast(FP8X4),
                     scales=tok_scale[SCALE_ROWS * a : P, lo:hi],
-                    in_=woven[:].rearrange("p w t -> p (w t)"),
+                    in_=woven[:].rearrange("p t d -> p (t d)"),
                 )
             if a == 0:
-                gather_codes(0, 0)
-                gather_codes(0, 1)
+                gather_codes(0, 0, "slot_codes00")
 
-        for h in range(2):
-            nc.vector.tensor_copy(slot_scale[h][:], tok_scale[:].indirect(listed(*PARTS[h])))
-            if h == 0:
-                for q in range(4):
-                    nc.scalar.dma_start(
-                        moved_scale[h][32 * q : 32 * q + SCALE_ROWS, :].bitcast(I32),
-                        slot_scale[h][32 * q + SCALE_ROWS : 32 * q + 2 * SCALE_ROWS, :].bitcast(I32),
-                    )
-            else:
-                nc.sync.dma_start(
-                    moved_scale[h][0:SHIFT_PARTS, :].bitcast(I32),
-                    slot_scale[h][SCALE_ROWS : SCALE_ROWS + SHIFT_PARTS, :].bitcast(I32),
-                )
-        load_weights(1, "then_weights")
-        for h in range(2):
-            gather_codes(1, h)
-        load_gate(1, "then_gate1")
+        gather_scales(0)
+        for r in range(SCALE_ROWS):
+            nc.scalar.dma_start(
+                moved_scale[0][r:P:QUADRANT, :].bitcast(I32),
+                slot_scale[0][SCALE_ROWS + r : P : QUADRANT, :].bitcast(I32),
+            )
+        gather_codes(1, 0, "slot_codes10")
+        gather_scales(1)
+        nc.sync.dma_start(
+            moved_scale[1][0:MOVE_PARTITIONS, :].bitcast(I32),
+            slot_scale[1][SCALE_ROWS : SCALE_ROWS + MOVE_PARTITIONS, :].bitcast(I32),
+        )
+        gather_codes(0, 1, f"woven{PASSES - 1}{len(CHUNKS) - 1}")
+        gather_codes(1, 1, "slot_codes11")
+        load_weights(1, "tok_scale")
+        load_gate(1, "tok_codes1")
 
-        squared = [[keep.tile([P, hi - lo], F32, name=f"squared{c}{h}") for h, (lo, hi) in enumerate(PARTS)] for c in range(BLOCKS)]
-        windows = [keep.tile([P, WIDE_WINDOW], F32, name=f"window{c}") for c in range(BLOCKS)]
+        squared = [
+            [keep.tile([P, hi - lo], F32, name=f"squared{c}{h}") for h, (lo, hi) in enumerate(PARTS)]
+            for c in range(BLOCKS)
+        ]
+        windows = [keep.tile([P, WINDOW], F32, name=f"window{c}") for c in range(BLOCKS)]
 
-        def expert(e, c):
+        def expert(e, c, bank_width):
             h = min(e, 1)
             first = e * C - PARTS[h][0]
-            width = GROUP if (e, c) == (0, 0) else C
             relu = keep.tile([P, C], F32, name=f"relu{e}{c}")
-            for s in range(0, C, GROUP):
-                if s % width == 0:
-                    bank = psum.tile([P, width], F32, name=f"bank{width}")
-                cols = slice(first + s, first + s + GROUP)
-                for a in range(PASSES):
-                    scales = slot_scale[h] if a == 0 else moved_scale[h]
-                    nc.tensor.matmul_mx(
-                        out=bank[:, s % width : s % width + GROUP],
-                        lhsT=w_code[h][:, first // C * PASSES + a, 2 * P * c : 2 * P * (c + 1)].bitcast(FP4X4),
-                        lhsT_scale=w_scale[:, e * PASSES + a, P * c : P * (c + 1)],
-                        rhs=slot_codes[a][h][:, cols].bitcast(FP8X4),
-                        rhs_scale=scales[:, cols],
-                        start=(a == 0),
-                        stop=(a == PASSES - 1),
-                    )
-                if (s + GROUP) % width == 0:
-                    nc.scalar.activation(
-                        relu[:, s + GROUP - width : s + GROUP], bank[:], ACT.Relu, bias=bias[:, c, e : e + 1]
-                    )
+            for lo in range(0, C, bank_width):
+                bank = psum.tile([P, bank_width], F32, name=f"bank{bank_width}")
+                for s in range(lo, lo + bank_width, GROUP):
+                    for a in range(PASSES):
+                        scales = slot_scale[h] if a == 0 else moved_scale[h]
+                        nc.tensor.matmul_mx(
+                            out=bank[:, s - lo : s - lo + GROUP],
+                            lhsT=w_code[h][:, first // C * PASSES + a, 2 * P * c : 2 * P * (c + 1)].bitcast(FP4X4),
+                            lhsT_scale=w_scale[:, e * PASSES + a, P * c : P * (c + 1)],
+                            rhs=codes_of(a, e * C + s).bitcast(FP8X4),
+                            rhs_scale=scales[:, first + s : first + s + GROUP],
+                            start=(a == 0),
+                            stop=(a == PASSES - 1),
+                        )
+                nc.scalar.activation(relu[:, lo : lo + bank_width], bank[:], ACT.Relu, bias=bias[:, c, e : e + 1])
             nc.scalar.activation(squared[c][h][:, first : first + C], relu[:], ACT.Square)
 
         def scatter(c, h):
-            lo, hi = PARTS[h]
-            nc.vector.tensor_tensor(windows[c][:].indirect(listed(lo, hi)), squared[c][h][:], gate_sb[h][:], MULT)
+            nc.vector.tensor_tensor(
+                windows[c][:].indirect(listed(*PARTS[h])), squared[c][h][:], gate_sb[h][:], MULT
+            )
 
         for c in range(BLOCKS):
-            expert(0, c)
+            expert(0, c, GROUP if c == 0 else C)
             scatter(c, 0)
         for c in range(BLOCKS):
             for e in range(1, E):
-                expert(e, c)
+                expert(e, c, C)
             scatter(c, 1)
             nc.sync.dma_start(out[c * P : (c + 1) * P, :], windows[c][:, 0:T])

@@ -34,7 +34,6 @@ VECTOR_TOKENS = ((256, 128, 64), (0, 64, 128))
 PARTS = ((0, C), (C, SLOTS))
 CODE_PARTS = (((0, 3 * C), (3 * C, SLOTS)), PARTS)
 WINDOW = 2 * (SLOTS - C)
-MOVE_PARTITIONS = 112
 PSUM_BUFS = 3
 
 
@@ -121,8 +120,13 @@ def tile_moe_pad_lin_relu2_kernel(tc, xT, w_words, w_scales, b, gate, offs, out)
             slot_codes[a, h] = keep.tile([P, hi - lo], U32, name=f"slot_codes{a}{h}", tag=tag, align_bytes=64)
             nc.vector.tensor_copy(slot_codes[a, h][:], tok_codes[a][:].indirect(listed(lo, hi)))
 
-        def gather_scales(h):
+        def gather_scales(h, queue):
             nc.vector.tensor_copy(slot_scale[h][:], tok_scale[:].indirect(listed(*PARTS[h])))
+            for r in range(SCALE_ROWS):
+                queue.dma_start(
+                    moved_scale[h][r:P:QUADRANT, :].bitcast(I32),
+                    slot_scale[h][SCALE_ROWS + r : P : QUADRANT, :].bitcast(I32),
+                )
 
         def codes_of(a, slot):
             h = 0 if slot < CODE_PARTS[a][0][1] else 1
@@ -145,18 +149,9 @@ def tile_moe_pad_lin_relu2_kernel(tc, xT, w_words, w_scales, b, gate, offs, out)
             if a == 0:
                 gather_codes(0, 0, "slot_codes00")
 
-        gather_scales(0)
-        for r in range(SCALE_ROWS):
-            nc.scalar.dma_start(
-                moved_scale[0][r:P:QUADRANT, :].bitcast(I32),
-                slot_scale[0][SCALE_ROWS + r : P : QUADRANT, :].bitcast(I32),
-            )
+        gather_scales(0, nc.scalar)
         gather_codes(1, 0, "slot_codes10")
-        gather_scales(1)
-        nc.sync.dma_start(
-            moved_scale[1][0:MOVE_PARTITIONS, :].bitcast(I32),
-            slot_scale[1][SCALE_ROWS : SCALE_ROWS + MOVE_PARTITIONS, :].bitcast(I32),
-        )
+        gather_scales(1, nc.sync)
         gather_codes(0, 1, f"woven{PASSES - 1}{len(CHUNKS) - 1}")
         gather_codes(1, 1, "slot_codes11")
         load_weights(1, "tok_scale")

from contextlib import ExitStack

import concourse.mybir as mybir

K, T, E, C, N = 1024, 640, 4, 256, 512
SLOTS = E * C
FLOPS = 2 * K * N * SLOTS

F32 = mybir.dt.float32
BF16 = mybir.dt.bfloat16
I32 = mybir.dt.int32
U32 = mybir.dt.uint32
U16 = mybir.dt.uint16
U8 = mybir.dt.uint8
FP8X4 = mybir.dt.float8_e4m3fn_x4
FP4X4 = mybir.dt.float4_e2m1fn_x4
ACT = mybir.ActivationFunctionType
MULT = mybir.AluOpType.mult

P = 128
QUADRANT = 32
SCALE_ROWS = 4
PACK = 4
K_PASS = P * PACK
PASSES = K // K_PASS
BLOCKS = N // P
GROUP = 128
LIST_ROWS = 16
LINE = 4
BIAS_PITCH = 8

CHUNKS = ((0, 256), (256, 512), (512, 640))
VECTOR_TOKENS = ((256, 128, 64), (0, 64, 128))
PARTS = ((0, C), (C, SLOTS))
CODE_PARTS = (((0, 3 * C), (3 * C, SLOTS)), PARTS)
WINDOW = 2 * (SLOTS - C)
PSUM_BUFS = 3


def tile_moe_pad_lin_relu2_kernel(tc, xT, w_words, w_scales, b, gate, offs, out):
    nc = tc.nc
    with ExitStack() as ctx:
        keep = ctx.enter_context(tc.tile_pool(name="keep", bufs=1))
        psum = ctx.enter_context(tc.psum_pool(name="psum", bufs=PSUM_BUFS))

        offsets = keep.tile([P, SLOTS // LIST_ROWS], U16, name="offsets")

        def listed(lo, hi):
            return offsets[:, lo // LIST_ROWS : hi // LIST_ROWS]

        w_scale = keep.tile([P, E * PASSES, N], U8, name="w_scale", align_bytes=64)
        nc.vector.memset(w_scale[:].rearrange("p g n -> p (g n)").bitcast(I32), 0)
        tok_scale = keep.tile([P, SLOTS], U8, name="tok_scale", tag="tok_scale", align_bytes=64)
        nc.vector.memset(tok_scale[:].bitcast(I32), 0)
        tok_codes = [
            keep.tile([P, SLOTS], U32, name=f"tok_codes{a}", tag=f"tok_codes{a}", align_bytes=64) for a in range(PASSES)
        ]
        for a in range(PASSES):
            nc.vector.memset(tok_codes[a][:, T:].bitcast(I32), 0)
        moved_scale = [
            keep.tile([P, hi - lo], U8, name=f"moved_scale{h}", align_bytes=64) for h, (lo, hi) in enumerate(PARTS)
        ]
        for h in range(len(PARTS)):
            nc.vector.memset(moved_scale[h][:].bitcast(I32), 0)

        warm = keep.tile([P, 8], F32, name="warm")
        nc.gpsimd.memset(warm[:], 0.0)
        warm_out = keep.tile([P, 8], F32, name="warm_out")
        nc.scalar.activation(warm_out[:], warm[:], ACT.Square)

        raw = {}
        for a in range(PASSES):
            rows = xT[a * K_PASS : (a + 1) * K_PASS, :].rearrange("(p d) t -> p d t", d=PACK)
            for i, (lo, hi) in enumerate(CHUNKS):
                raw[a, i] = keep.tile([P, PACK, hi - lo], F32, name=f"raw{a}{i}")
                nc.sync.dma_start(raw[a, i][:], rows[:, :, lo:hi])
            if a == 0:
                nc.sync.dma_start(offsets[:], offs)
        for r in range(SCALE_ROWS):
            nc.sync.dma_start(
                w_scale[r:P:QUADRANT, :, :].bitcast(I32),
                w_scales.rearrange("e a (q r) n -> r q (e a) n", r=SCALE_ROWS)[r].bitcast(I32),
            )

        w_code, gate_sb = {}, {}

        def load_weights(h, tag):
            lo, hi = PARTS[h]
            w_code[h] = keep.tile([P, (hi - lo) // C * PASSES, 2 * N], U8, name=f"w_code{h}", tag=tag, align_bytes=64)
            nc.sync.dma_start(
                w_code[h][:].bitcast(I32),
                w_words[lo // C : hi // C].rearrange("e a p n -> p (e a) n").bitcast(I32),
            )

        def load_gate(h, tag):
            lo, hi = PARTS[h]
            gate_sb[h] = keep.tile([P, hi - lo], F32, name=f"gate{h}", tag=tag, align_bytes=64)
            nc.sync.dma_start(gate_sb[h][:], gate[0:P, lo:hi])

        load_weights(0, "w_code0")
        bias = keep.tile([P, BLOCKS, BIAS_PITCH], F32, name="bias")
        nc.sync.dma_start(bias[:, :, 0:E], b.rearrange("(c p) e -> p c e", p=P))
        load_gate(0, "gate0")

        def weave(on_vector, dst, src):
            dst_view = dst.rearrange("p (g i) d -> p g d i", i=LINE)
            src_view = src.rearrange("p d (g i) -> p g d i", i=LINE)
            if on_vector:
                nc.vector.tensor_copy(dst_view, src_view)
            else:
                nc.scalar.activation(dst_view, src_view, ACT.Copy)

        slot_codes = {}
        slot_scale = [
            keep.tile([P, hi - lo], U8, name=f"slot_scale{h}", align_bytes=64) for h, (lo, hi) in enumerate(PARTS)
        ]

        def gather_codes(a, h, tag):
            lo, hi = CODE_PARTS[a][h]
            slot_codes[a, h] = keep.tile([P, hi - lo], U32, name=f"slot_codes{a}{h}", tag=tag, align_bytes=64)
            nc.vector.tensor_copy(slot_codes[a, h][:], tok_codes[a][:].indirect(listed(lo, hi)))

        def gather_scales(h, queue):
            nc.vector.tensor_copy(slot_scale[h][:], tok_scale[:].indirect(listed(*PARTS[h])))
            for r in range(SCALE_ROWS):
                queue.dma_start(
                    moved_scale[h][r:P:QUADRANT, :].bitcast(I32),
                    slot_scale[h][SCALE_ROWS + r : P : QUADRANT, :].bitcast(I32),
                )

        def codes_of(a, slot):
            h = 0 if slot < CODE_PARTS[a][0][1] else 1
            first = slot - CODE_PARTS[a][h][0]
            return slot_codes[a, h][:, first : first + GROUP]

        for a in range(PASSES):
            for i, (lo, hi) in enumerate(CHUNKS):
                width, cut = hi - lo, VECTOR_TOKENS[a][i]
                woven = keep.tile([P, width, PACK], BF16, name=f"woven{a}{i}", tag=f"woven{a}{i}", align_bytes=64)
                if cut > 0:
                    weave(True, woven[:, 0:cut, :], raw[a, i][:, :, 0:cut])
                if cut < width:
                    weave(False, woven[:, cut:width, :], raw[a, i][:, :, cut:width])
                nc.vector.quantize_mx(
                    out=tok_codes[a][:, lo:hi].bitcast(FP8X4),
                    scales=tok_scale[SCALE_ROWS * a : P, lo:hi],
                    in_=woven[:].rearrange("p t d -> p (t d)"),
                )
            if a == 0:
                gather_codes(0, 0, "slot_codes00")

        gather_scales(0, nc.scalar)
        gather_codes(1, 0, "slot_codes10")
        gather_scales(1, nc.sync)
        gather_codes(0, 1, f"woven{PASSES - 1}{len(CHUNKS) - 1}")
        gather_codes(1, 1, "slot_codes11")
        load_weights(1, "tok_scale")
        load_gate(1, "tok_codes1")

        squared = [
            [keep.tile([P, hi - lo], F32, name=f"squared{c}{h}") for h, (lo, hi) in enumerate(PARTS)]
            for c in range(BLOCKS)
        ]
        windows = [keep.tile([P, WINDOW], F32, name=f"window{c}") for c in range(BLOCKS)]

        def expert(e, c, bank_width):
            h = min(e, 1)
            first = e * C - PARTS[h][0]
            relu = keep.tile([P, C], F32, name=f"relu{e}{c}")
            for lo in range(0, C, bank_width):
                bank = psum.tile([P, bank_width], F32, name=f"bank{bank_width}")
                for s in range(lo, lo + bank_width, GROUP):
                    for a in range(PASSES):
                        scales = slot_scale[h] if a == 0 else moved_scale[h]
                        nc.tensor.matmul_mx(
                            out=bank[:, s - lo : s - lo + GROUP],
                            lhsT=w_code[h][:, first // C * PASSES + a, 2 * P * c : 2 * P * (c + 1)].bitcast(FP4X4),
                            lhsT_scale=w_scale[:, e * PASSES + a, P * c : P * (c + 1)],
                            rhs=codes_of(a, e * C + s).bitcast(FP8X4),
                            rhs_scale=scales[:, first + s : first + s + GROUP],
                            start=(a == 0),
                            stop=(a == PASSES - 1),
                        )
                nc.scalar.activation(relu[:, lo : lo + bank_width], bank[:], ACT.Relu, bias=bias[:, c, e : e + 1])
            nc.scalar.activation(squared[c][h][:, first : first + C], relu[:], ACT.Square)

        def scatter(c, h):
            nc.vector.tensor_tensor(
                windows[c][:].indirect(listed(*PARTS[h])), squared[c][h][:], gate_sb[h][:], MULT
            )

        for c in range(BLOCKS):
            expert(0, c, GROUP if c == 0 else C)
            scatter(c, 0)
        for c in range(BLOCKS):
            for e in range(1, E):
                expert(e, c, C)
            scatter(c, 1)
            nc.sync.dma_start(out[c * P : (c + 1) * P, :], windows[c][:, 0:T])
